import numpy as np
import ml_dtypes


def mxq(x, axis, fmt="e4m3"):
    dtype, down = {"e4m3": (ml_dtypes.float8_e4m3fn, 7), "e5m2": (ml_dtypes.float8_e5m2, 14)}[fmt]
    v = np.moveaxis(np.asarray(x, np.float32).astype(ml_dtypes.bfloat16).astype(np.float64), axis, -1)
    blocks = v.reshape(v.shape[:-1] + (-1, 32))
    amax = np.abs(blocks).max(-1, keepdims=True)
    byte = np.maximum(np.where(amax > 0, np.frexp(amax)[1] - 1 + 127, 0) - down, 1)
    scale = np.exp2(byte - 127.0)
    codes = (blocks / scale).astype(np.float32).astype(dtype).astype(np.float64)
    return np.moveaxis((codes * scale).reshape(v.shape), -1, axis)


WIDE = False


def mx_kscale(k):
    if not WIDE:
        return np.ones(k)
    levels = np.array([10, -10, 5, -5, 0])
    if k % 512:
        return np.exp2(np.random.permutation(np.resize(levels, k // 32))).repeat(32)
    a = np.empty((k // 512, 16))
    for p in range(k // 512):
        a[p, :8] = np.random.permutation(np.resize(levels, 8))
        for g in range(8):
            far = levels[np.abs(levels - a[p, g]) >= 10]
            a[p, g + 8] = far[np.random.randint(len(far))]
    return np.exp2(a.ravel()).repeat(32)


BF16 = ml_dtypes.bfloat16


def bf(x):
    return np.asarray(x, np.float32).astype(BF16)


def f64(x):
    return np.asarray(x).astype(np.float64)


E2M1 = np.array([0.0, 0.5, 1.0, 1.5, 2.0, 3.0, 4.0, 6.0, -0.0, -0.5, -1.0, -1.5, -2.0, -3.0, -4.0, -6.0])


def pack_weight(w, fmt):
    k, n = w.shape
    w = f64(bf(w)).reshape(k // 32, 32, n)
    amax = np.abs(w).max(1)
    if fmt == "e4m3":
        byte = np.frexp(amax)[1] - 1 + 127 - 7
    else:
        mant, ex = np.frexp(amax / 6.0)
        byte = np.where(mant > 0.5, ex, ex - 1) + 127
    byte = np.clip(np.where(amax > 0, byte, 1), 1, 254)
    scaled = (w * np.exp2(127.0 - byte)[:, None, :]).reshape(k, n).astype(np.float32)
    by_word = np.ascontiguousarray(scaled.reshape(k // 512, 128, 4, n).transpose(0, 1, 3, 2))
    if fmt == "e4m3":
        words = by_word.astype(ml_dtypes.float8_e4m3fn).view(np.uint8)
    else:
        c = by_word.astype(ml_dtypes.float4_e2m1fn).view(np.uint8) & 0xF
        words = c[..., 0::2] | (c[..., 1::2] << 4)
    return np.ascontiguousarray(words), np.ascontiguousarray(byte.astype(np.uint8).reshape(k // 512, 16, n))


def unpack_weight(words, scales, fmt):
    g, p, n, _ = words.shape
    if fmt == "e4m3":
        vals = np.ascontiguousarray(words).view(ml_dtypes.float8_e4m3fn).astype(np.float64)
    else:
        nib = np.empty((g, p, n, 4), np.uint8)
        nib[..., 0::2] = words & 0xF
        nib[..., 1::2] = words >> 4
        vals = E2M1[nib]
    vals = vals * np.repeat(np.exp2(scales.astype(np.float64) - 127.0), 8, axis=1)[..., None]
    return vals.transpose(0, 1, 3, 2).reshape(g * 512, n)


B, D, H, C = 1024, 1024, 1024, 512


def draw0():
    s, t = mx_kscale(D), mx_kscale(H)
    x = bf(np.random.standard_normal((B, D)) * s)
    w1_words, w1_scales = pack_weight(np.random.standard_normal((D, H)) * 1.2 / np.sqrt(D) / s[:, None], "e4m3")
    g1 = bf((1.0 + 0.1 * np.random.standard_normal(H)) * t)
    v1_words, v1_scales = pack_weight(np.random.standard_normal((H, C)) / np.sqrt(H) / t[:, None], "e4m3")
    wx_words, wx_scales = pack_weight(np.random.standard_normal((D, C)) * 0.8 / np.sqrt(D) / s[:, None], "e4m3")
    wh_words, wh_scales = pack_weight(np.random.standard_normal((H, C)) * 1.2 / np.sqrt(H) / t[:, None], "e4m3")
    u = bf(np.random.standard_normal((B, C)))
    return {
        "x": x,
        "w1_words": w1_words,
        "w1_scales": w1_scales,
        "g1": g1,
        "v1_words": v1_words,
        "v1_scales": v1_scales,
        "wx_words": wx_words,
        "wx_scales": wx_scales,
        "wh_words": wh_words,
        "wh_scales": wh_scales,
        "u": u,
    }


def centred_features(xq, w1_words, w1_scales, g1):
    r = np.maximum(xq @ unpack_weight(w1_words, w1_scales, "e4m3"), 0.0)
    return (r - np.mean(r, axis=0, keepdims=True)) * f64(g1)[None, :]


def newton_target(y, score):
    return y * (1.0 + np.exp(-y * score))


def core(x, w1_words, w1_scales, g1, v1_words, v1_scales, wx_words, wx_scales, wh_words, wh_scales, u):
    xq = mxq(f64(x), 1, "e4m3")
    h = centred_features(xq, w1_words, w1_scales, g1)
    hq = mxq(h, 1, "e4m3")
    s1 = hq @ unpack_weight(v1_words, v1_scales, "e4m3")
    p = (xq @ unpack_weight(wx_words, wx_scales, "e4m3")) + (hq @ unpack_weight(wh_words, wh_scales, "e4m3"))
    score = 0.8 * s1 + 0.8 * np.tanh(p)
    y = np.where(f64(u) < 0, -1.0, 1.0)
    return newton_target(y, score)


def e4m3fn_bytes(y):
    return np.clip(np.asarray(y, np.float64), -448.0, 448.0).astype(np.float32).astype(ml_dtypes.float8_e4m3fn).view(np.uint8)


def e4m3fn_values(b):
    return np.asarray(b, np.uint8).view(ml_dtypes.float8_e4m3fn).astype(np.float64)


def setup_inputs():
    d = draw0()
    x0 = np.asarray(d['x']).astype(np.float64)
    s = (np.max(np.abs(x0), axis=(0,), keepdims=True) / 448.0).astype(np.float32)
    out = {}
    for k, v in d.items():
        if k == 'x':
            out['x_bytes'] = e4m3fn_bytes(x0 / s.astype(np.float64))
            out['x_scale'] = s
        else:
            out[k] = v
    return out


def reference(x_bytes, x_scale, w1_words, w1_scales, g1, v1_words, v1_scales, wx_words, wx_scales, wh_words, wh_scales, u):
    return core(e4m3fn_values(x_bytes) * x_scale.astype(np.float64), w1_words, w1_scales, g1, v1_words, v1_scales, wx_words, wx_scales, wh_words, wh_scales, u)

@@ -1,0 +1,395 @@
+import math
+from contextlib import ExitStack
+
+import concourse.mybir as mybir
+from concourse.masks import make_identity
+
+F32 = mybir.dt.float32
+BF16 = mybir.dt.bfloat16
+I32 = mybir.dt.int32
+U32 = mybir.dt.uint32
+U8 = mybir.dt.uint8
+FP8 = mybir.dt.float8_e4m3fn
+FP8X4 = mybir.dt.float8_e4m3fn_x4
+ALU = mybir.AluOpType
+ACT = mybir.ActivationFunctionType
+AX = mybir.AxisListType
+
+P = 128
+B, D, H, C = 1024, 1024, 1024, 512
+RT = B // P
+KG = D // 512
+FLOPS = 2 * B * D * H + 3 * 2 * B * H * C
+
+CHUNKS = ((0, 256), (256, 256), (512, 256), (768, 256))
+
+
+def tile_grownetnewtontargets_w8_kernel(
+    tc, x_bytes, x_scale, w1_words, w1_scales, g1, v1_words, v1_scales, wx_words, wx_scales, wh_words, wh_scales, u, out
+):
+    nc = tc.nc
+    with ExitStack() as ctx:
+        keep = ctx.enter_context(tc.tile_pool(name="keep", bufs=1))
+        work = ctx.enter_context(tc.tile_pool(name="work", bufs=4))
+        psum = ctx.enter_context(tc.psum_pool(name="psum", bufs=1))
+
+        xu = keep.tile([P, RT, D], U8, align_bytes=64)
+        sc = keep.tile([P, D], F32, align_bytes=64)
+        w1raw = keep.tile([P, KG, H], I32, align_bytes=64)
+        w1p = keep.tile([P, KG, H], I32, align_bytes=64)
+        w1s = keep.tile([P, H], U8, align_bytes=64)
+        w1sp = keep.tile([P, H], U8, align_bytes=64)
+        w2 = {}
+        w2s = {}
+        wsrc = {"x": (wx_words, wx_scales), "v": (v1_words, v1_scales), "h": (wh_words, wh_scales)}
+        for n in ("x", "v", "h"):
+            w2[n] = keep.tile([P, KG, C], I32, align_bytes=64, name="w2" + n)
+            w2s[n] = keep.tile([P, C], U8, align_bytes=64, name="w2s" + n)
+        g1b = keep.tile([P, KG, 4], BF16, align_bytes=64)
+        g1f = keep.tile([P, KG * 4], F32, align_bytes=64)
+        ut = keep.tile([P, RT, C], BF16, align_bytes=64)
+        yh = keep.tile([P, RT, C], BF16, align_bytes=64)
+        ident = keep.tile([P, P], F32, align_bytes=64)
+        identb = keep.tile([P, P], BF16, align_bytes=64)
+        dummy = keep.tile([P, 1], F32, align_bytes=64)
+        dummy2 = keep.tile([P, 1], F32, align_bytes=64)
+        xc = keep.tile([P, KG, B], U32, align_bytes=64)
+        xs = keep.tile([P, KG, B], U8, align_bytes=64)
+        r32 = keep.tile([P, 8, B], F32, align_bytes=64)
+        hp = keep.tile([P, 8, B], BF16, align_bytes=64)
+        sums = keep.tile([P, 8, len(CHUNKS)], F32, align_bytes=64)
+        mean = keep.tile([P, 8], F32, align_bytes=64)
+        part = keep.tile([P, 8], F32, align_bytes=64)
+        hc = keep.tile([P, KG, B], U32, align_bytes=64)
+        hs = keep.tile([P, KG, B], U8, align_bytes=64)
+
+        nc.vector.memset(dummy[:], 0.0)
+        nc.scalar.activation(out=dummy2[:], in_=dummy[:], func=ACT.Exp)
+        nc.vector.memset(w1s[:].bitcast(I32), 0)
+        for n in ("x", "v", "h"):
+            nc.gpsimd.memset(w2s[n][:].bitcast(I32), 0)
+        make_identity(nc, ident[:])
+        make_identity(nc, identb[:])
+
+        xv = x_bytes.rearrange("(p r) k -> p r k", r=RT)
+        sv = x_scale.rearrange("o k -> (o k)")
+
+        def load_x(r0, r1):
+            nc.sync.dma_start(out=xu[:, r0:r1, :], in_=xv[:, r0:r1, :])
+
+        nc.sync.dma_start(out=sc[:, 0:512], in_=sv[0:512].partition_broadcast(P))
+        load_x(0, 1)
+        nc.sync.dma_start(out=sc[:, 512:1024], in_=sv[512:1024].partition_broadcast(P))
+        load_x(1, 2)
+        for q in range(4):
+            nc.sync.dma_start(
+                out=w1s[32 * q : 32 * q + 8, :].bitcast(I32), in_=w1_scales[:, 4 * q : 4 * q + 4, :].bitcast(I32)
+            )
+        for g in range(KG):
+            nc.sync.dma_start(
+                out=w1raw[:, g, :], in_=w1_words[g].rearrange("p n t -> p (n t)").bitcast(I32)
+            )
+        load_x(2, 4)
+        load_x(4, 8)
+        nc.scalar.dma_start(out=g1b[:], in_=g1.rearrange("(g p t) -> p g t", g=KG, t=4))
+        nc.sync.dma_start(out=ut[:], in_=u.rearrange("(p r) c -> p r c", r=RT))
+        for n in ("x", "h", "v"):
+            words, scales = wsrc[n]
+            for q in range(4):
+                nc.sync.dma_start(
+                    out=w2s[n][32 * q : 32 * q + 8, :].bitcast(I32), in_=scales[:, 4 * q : 4 * q + 4, :].bitcast(I32)
+                )
+            for g in range(KG):
+                nc.sync.dma_start(
+                    out=w2[n][:, g, :], in_=words[g].rearrange("p n t -> p (n t)").bitcast(I32)
+                )
+
+        turn = [0]
+
+        def rotate():
+            turn[0] = (turn[0] + 1) % 8
+            return turn[0]
+
+        def bank_f32(k):
+            return psum.tile([P, 512], F32, name="bank%d" % k)
+
+        xT = {}
+
+        xbs = {}
+
+        def product(r):
+            xb = work.tile([P, D], BF16, align_bytes=64, name="xb")
+            n = 512 if r == 0 else 1024
+            for c in range(0, D, n):
+                nc.vector.tensor_tensor(
+                    out=xb[:, c : c + n], in0=xu[:, r, c : c + n].bitcast(FP8), in1=sc[:, c : c + n], op=ALU.mult
+                )
+            xbs[r] = xb
+
+        def turn_x(r):
+            words = xbs[r][:].bitcast(F32)
+            bank = bank_f32(rotate())
+            for g in range(KG):
+                for w in range(2):
+                    i = 2 * g + w
+                    nc.tensor.transpose(
+                        bank[:, 128 * i : 128 * i + 128], words[:, 256 * g + w : 256 * (g + 1) : 2], ident[:]
+                    )
+            if r % 2 == 0:
+                xT[r // 2] = work.tile([P, KG * 256 * 4], BF16, align_bytes=64, name="xTt")
+            dst = xT[r // 2][:].bitcast(F32).rearrange("p (g n w) -> p g n w", g=KG, w=2)
+            i = r % 2
+            nc.scalar.copy(
+                out=dst[:, :, 128 * i : 128 * i + 128, :], in_=bank[:].rearrange("p (g w n) -> p g n w", g=KG, w=2)
+            )
+
+        def quant_x(pair):
+            for g in range(KG):
+                cols = slice(256 * pair, 256 * pair + 256)
+                nc.vector.quantize_mx(
+                    out=xc[:, g, cols].bitcast(FP8X4), scales=xs[:, g, cols], in_=xT[pair][:, 1024 * g : 1024 * g + 1024]
+                )
+
+        def permute_w1(g):
+                nc.vector.tensor_copy(
+                    out=w1p[:, g, :].rearrange("p (c t m) -> p c t m", c=2, t=4),
+                    in_=w1raw[:, g, :].rearrange("p (c m t) -> p c t m", c=2, t=4),
+                )
+
+        def permute_w1_scales():
+            nc.vector.tensor_copy(
+                out=w1sp[:].rearrange("p (c t m) -> p c t m", c=2, t=4),
+                in_=w1s[:].rearrange("p (c m t) -> p c t m", c=2, t=4),
+            )
+
+        def stage1(ci, j, on_vector=False):
+            c0, n = CHUNKS[ci]
+            bank = bank_f32(rotate())
+            for g in range(KG):
+                nc.tensor.matmul_mx(
+                    out=bank[:, :n],
+                    lhsT=w1p[:, g, 128 * j : 128 * j + 128].bitcast(FP8X4),
+                    lhsT_scale=w1sp[4 * g : P, 128 * j : 128 * j + 128],
+                    rhs=xc[:, g, c0 : c0 + n].bitcast(FP8X4),
+                    rhs_scale=xs[:, g, c0 : c0 + n],
+                    start=(g == 0),
+                    stop=(g == KG - 1),
+                )
+            acc = sums[:, j, ci : ci + 1]
+            if on_vector:
+                nc.vector.tensor_scalar(
+                    out=r32[:, j, c0 : c0 + n], in0=bank[:, :n], scalar1=0.0, scalar2=None, op0=ALU.max, op1=ALU.add,
+                    accum_out=acc,
+                )
+            else:
+                nc.scalar.activation(out=r32[:, j, c0 : c0 + n], in_=bank[:, :n], func=ACT.Relu, accum_out=acc)
+
+        def means_early():
+            nc.vector.reduce_sum(out=part[:], in_=sums[:, :, 0:3], axis=AX.X)
+            nc.vector.tensor_scalar(out=part[:], in0=part[:], scalar1=1.0 / B, scalar2=None, op0=ALU.mult)
+
+        def means(cg):
+            js = slice(4 * cg, 4 * cg + 4)
+            nc.vector.scalar_tensor_tensor(
+                out=mean[:, js], in0=sums[:, js, 3], scalar=1.0 / B, in1=part[:, js], op0=ALU.mult, op1=ALU.add
+            )
+
+        def centre(cg, half, ts=(0, 1, 2, 3)):
+            for t in ts:
+                j = 4 * cg + t
+                cols = slice(512 * half, 512 * half + 512)
+                nc.vector.tensor_scalar(
+                    out=hp[:, j, cols], in0=r32[:, j, cols], scalar1=mean[:, j : j + 1],
+                    scalar2=g1f[:, j : j + 1], op0=ALU.subtract, op1=ALU.mult,
+                )
+
+        hi = {}
+
+        def inter(cg, blk, bk):
+            hi[cg, blk] = keep.tile([P, 1024], BF16, align_bytes=64, name="hi%d%d" % (cg, blk))
+            bank = psum.tile([P, 1024], BF16, name="bank%d" % bk)
+            for k in range(2):
+                n0 = 256 * blk + 128 * k
+                nc.tensor.matmul(
+                    out=bank[:, 512 * k : 512 * k + 512].rearrange("p (n t) -> p n t", t=4),
+                    lhsT=identb[:],
+                    rhs=hp[:, 4 * cg : 4 * cg + 4, n0 : n0 + 128].rearrange("p t n -> p n t"),
+                    start=True,
+                    stop=True,
+                )
+            nc.scalar.copy(out=hi[cg, blk][:], in_=bank[:])
+
+        def quant_h(cg, blk):
+                cols = slice(256 * blk, 256 * blk + 256)
+                nc.vector.quantize_mx(out=hc[:, cg, cols].bitcast(FP8X4), scales=hs[:, cg, cols], in_=hi[cg, blk][:])
+
+        pbank = {}
+        sbank = {}
+
+        def mm(bank, codes, scales, g, b, n, start, stop):
+            nc.tensor.matmul_mx(
+                out=bank[:],
+                lhsT=codes[:, g, 128 * b : 128 * b + 128].bitcast(FP8X4),
+                lhsT_scale=scales[:, g, 128 * b : 128 * b + 128],
+                rhs=w2[n][:, g, :].bitcast(FP8X4),
+                rhs_scale=w2s[n][4 * g : P, :],
+                start=start,
+                stop=stop,
+            )
+
+        def px(b):
+            pbank[b] = bank_f32(b % 4)
+            for g in range(KG):
+                mm(pbank[b], xc, xs, g, b, "x", g == 0, False)
+
+        th = {}
+        ee = {}
+
+        def stage2(b, bk):
+            for g in range(KG):
+                mm(pbank[b], hc, hs, g, b, "h", False, g == KG - 1)
+            th[b] = work.tile([P, C], F32, align_bytes=64, name="tht")
+            nc.scalar.activation(out=th[b][:], in_=pbank[b][:], func=ACT.Tanh)
+            sbank[b] = bank_f32(bk)
+            for g in range(KG):
+                mm(sbank[b], hc, hs, g, b, "v", g == 0, g == KG - 1)
+
+        qq = {}
+
+        def epi_add(b, c0=0, c1=C):
+            qq[b, c0] = work.tile([P, C], F32, align_bytes=64, name="qt")
+            nc.vector.tensor_tensor(
+                out=qq[b, c0][:, : c1 - c0], in0=sbank[b][:, c0:c1], in1=th[b][:, c0:c1], op=ALU.add
+            )
+
+        def epi_exp(b, c0=0, c1=C):
+            n = c1 - c0
+            w = work.tile([P, C], F32, align_bytes=64, name="wt")
+            nc.vector.tensor_tensor(out=w[:, :n], in0=qq[b, c0][:, :n], in1=yh[:, b, c0:c1], op=ALU.mult)
+            ee[b, c0] = work.tile([P, C], F32, align_bytes=64, name="et")
+            nc.scalar.activation(out=ee[b, c0][:, :n], in_=w[:, :n], func=ACT.Exp, scale=-1.6, bias=math.log(2.0))
+
+        ov = out.rearrange("(p r) c -> p r c", r=RT)
+
+        def epi_out(b, c0=0, c1=C):
+            n = c1 - c0
+            o = work.tile([P, C], F32, align_bytes=64, name="ot")
+            nc.vector.scalar_tensor_tensor(
+                out=o[:, :n], in0=ee[b, c0][:, :n], scalar=2.0, in1=yh[:, b, c0:c1], op0=ALU.add, op1=ALU.mult
+            )
+            nc.sync.dma_start(out=ov[:, b, c0:c1], in_=o[:, :n])
+
+        def signs(r0, r1):
+            nc.vector.tensor_scalar(
+                out=yh[:, r0:r1, :], in0=ut[:, r0:r1, :], scalar1=0.0, scalar2=0.5, op0=ALU.is_ge, op1=ALU.subtract
+            )
+
+        product(0)
+        turn_x(0)
+        product(1)
+        turn_x(1)
+        permute_w1_scales()
+        permute_w1(0)
+        quant_x(0)
+        permute_w1(1)
+        product(2)
+        turn_x(2)
+        nc.vector.tensor_copy(out=g1f[:], in_=g1b[:].rearrange("p g t -> p (g t)"))
+        for j in range(3):
+            stage1(0, j)
+        product(3)
+        turn_x(3)
+        for j in range(3, 6):
+            stage1(0, j)
+        product(4)
+        quant_x(1)
+        turn_x(4)
+        for j in range(6, 8):
+            stage1(0, j)
+        for j in range(2):
+            stage1(1, j)
+        product(5)
+        turn_x(5)
+        for j in range(2, 5):
+            stage1(1, j)
+        product(6)
+        quant_x(2)
+        turn_x(6)
+        for j in range(5, 8):
+            stage1(1, j)
+        product(7)
+        turn_x(7)
+        for j in range(6):
+            stage1(2, j)
+        signs(0, 8)
+        quant_x(3)
+        stage1(2, 6, True)
+        stage1(2, 7, True)
+        means_early()
+        for j in range(4):
+            stage1(3, j)
+            stage1(3, 4 + j, True)
+        for b in range(4):
+            px(b)
+        means(0)
+        means(1)
+        centre(0, 0)
+        inter(0, 0, 4)
+        inter(0, 1, 5)
+        centre(1, 0)
+        inter(1, 0, 6)
+        inter(1, 1, 7)
+        centre(0, 1, (0, 1))
+        quant_h(0, 0)
+        centre(0, 1, (2, 3))
+        quant_h(1, 0)
+        centre(1, 1)
+        quant_h(0, 1)
+        quant_h(1, 1)
+        stage2(0, 4)
+        stage2(1, 5)
+        inter(0, 2, 6)
+        inter(1, 2, 7)
+        epi_add(0)
+        epi_add(1)
+        epi_exp(0)
+        epi_exp(1)
+        inter(0, 3, 4)
+        inter(1, 3, 5)
+        quant_h(0, 2)
+        quant_h(1, 2)
+        stage2(2, 6)
+        stage2(3, 7)
+        epi_out(0)
+        quant_h(0, 3)
+        epi_out(1)
+        quant_h(1, 3)
+        px(4)
+        stage2(4, 4)
+        px(5)
+        stage2(5, 5)
+        epi_add(2)
+        epi_add(3)
+        epi_exp(2)
+        epi_exp(3)
+        px(6)
+        stage2(6, 6)
+        px(7)
+        stage2(7, 7)
+        epi_add(4)
+        epi_out(2)
+        epi_exp(4)
+        epi_add(5)
+        epi_out(3)
+        epi_exp(5)
+        epi_add(6)
+        epi_out(4)
+        epi_exp(6)
+        epi_add(7, 0, 256)
+        epi_add(7, 256, 512)
+        epi_exp(7, 0, 256)
+        epi_exp(7, 256, 512)
+        epi_out(5)
+        epi_out(6)
+        epi_out(7, 0, 256)
+        epi_out(7, 256, 512)

@@ -20,8 +20,7 @@ B, D, H, C = 1024, 1024, 1024, 512
 RT = B // P
 KG = D // 512
 FLOPS = 2 * B * D * H + 3 * 2 * B * H * C
-
-CHUNKS = ((0, 256), (256, 256), (512, 256), (768, 256))
+HALF = C // 2
 
 
 def tile_grownetnewtontargets_w8_kernel(
@@ -32,8 +31,10 @@ def tile_grownetnewtontargets_w8_kernel(
         keep = ctx.enter_context(tc.tile_pool(name="keep", bufs=1))
         work = ctx.enter_context(tc.tile_pool(name="work", bufs=4))
         psum = ctx.enter_context(tc.psum_pool(name="psum", bufs=1))
+        ctx.enter_context(tc.manual_schedule())
 
         xu = keep.tile([P, RT, D], U8, align_bytes=64)
+        xsc = keep.tile([P, KG * 4], F32, align_bytes=64)
         sc = keep.tile([P, D], F32, align_bytes=64)
         w1raw = keep.tile([P, KG, H], I32, align_bytes=64)
         w1p = keep.tile([P, KG, H], I32, align_bytes=64)
@@ -41,8 +42,7 @@ def tile_grownetnewtontargets_w8_kernel(
         w1sp = keep.tile([P, H], U8, align_bytes=64)
         w2 = {}
         w2s = {}
-        wsrc = {"x": (wx_words, wx_scales), "v": (v1_words, v1_scales), "h": (wh_words, wh_scales)}
-        for n in ("x", "v", "h"):
+        for n in ("x", "h", "v"):
             w2[n] = keep.tile([P, KG, C], I32, align_bytes=64, name="w2" + n)
             w2s[n] = keep.tile([P, C], U8, align_bytes=64, name="w2s" + n)
         g1b = keep.tile([P, KG, 4], BF16, align_bytes=64)
@@ -57,86 +57,104 @@ def tile_grownetnewtontargets_w8_kernel(
         xs = keep.tile([P, KG, B], U8, align_bytes=64)
         r32 = keep.tile([P, 8, B], F32, align_bytes=64)
         hp = keep.tile([P, 8, B], BF16, align_bytes=64)
-        sums = keep.tile([P, 8, len(CHUNKS)], F32, align_bytes=64)
-        mean = keep.tile([P, 8], F32, align_bytes=64)
+        sums = keep.tile([P, 8, 4], F32, align_bytes=64)
         part = keep.tile([P, 8], F32, align_bytes=64)
+        mean = keep.tile([P, 8], F32, align_bytes=64)
+        shift = keep.tile([P, 8], F32, align_bytes=64)
         hc = keep.tile([P, KG, B], U32, align_bytes=64)
         hs = keep.tile([P, KG, B], U8, align_bytes=64)
 
+        make_identity(nc, ident[:])
         nc.vector.memset(dummy[:], 0.0)
+        nc.scalar.dma_start(out=xsc[:], in_=x_scale.rearrange("o (g p t) -> p (o g) t", g=KG, t=4))
         nc.scalar.activation(out=dummy2[:], in_=dummy[:], func=ACT.Exp)
         nc.vector.memset(w1s[:].bitcast(I32), 0)
-        for n in ("x", "v", "h"):
-            nc.gpsimd.memset(w2s[n][:].bitcast(I32), 0)
-        make_identity(nc, ident[:])
         make_identity(nc, identb[:])
+        for n in ("x", "h", "v"):
+            nc.vector.memset(w2s[n][:].bitcast(I32), 0)
+        nc.scalar.dma_start(out=g1b[:], in_=g1.rearrange("(g p t) -> p g t", g=KG, t=4))
 
         xv = x_bytes.rearrange("(p r) k -> p r k", r=RT)
-        sv = x_scale.rearrange("o k -> (o k)")
 
         def load_x(r0, r1):
             nc.sync.dma_start(out=xu[:, r0:r1, :], in_=xv[:, r0:r1, :])
 
-        nc.sync.dma_start(out=sc[:, 0:512], in_=sv[0:512].partition_broadcast(P))
-        load_x(0, 1)
-        nc.sync.dma_start(out=sc[:, 512:1024], in_=sv[512:1024].partition_broadcast(P))
-        load_x(1, 2)
-        for q in range(4):
-            nc.sync.dma_start(
-                out=w1s[32 * q : 32 * q + 8, :].bitcast(I32), in_=w1_scales[:, 4 * q : 4 * q + 4, :].bitcast(I32)
-            )
-        for g in range(KG):
-            nc.sync.dma_start(
-                out=w1raw[:, g, :], in_=w1_words[g].rearrange("p n t -> p (n t)").bitcast(I32)
-            )
-        load_x(2, 4)
-        load_x(4, 8)
-        nc.scalar.dma_start(out=g1b[:], in_=g1.rearrange("(g p t) -> p g t", g=KG, t=4))
-        nc.sync.dma_start(out=ut[:], in_=u.rearrange("(p r) c -> p r c", r=RT))
-        for n in ("x", "h", "v"):
-            words, scales = wsrc[n]
+        def load_scales(tile, scales):
             for q in range(4):
                 nc.sync.dma_start(
-                    out=w2s[n][32 * q : 32 * q + 8, :].bitcast(I32), in_=scales[:, 4 * q : 4 * q + 4, :].bitcast(I32)
+                    out=tile[32 * q : 32 * q + 8, :].bitcast(I32), in_=scales[:, 4 * q : 4 * q + 4, :].bitcast(I32)
                 )
+
+        def load_words(tile, words):
             for g in range(KG):
-                nc.sync.dma_start(
-                    out=w2[n][:, g, :], in_=words[g].rearrange("p n t -> p (n t)").bitcast(I32)
+                nc.sync.dma_start(out=tile[:, g, :], in_=words[g].rearrange("p n t -> p (n t)").bitcast(I32))
+
+        load_x(0, 2)
+        load_scales(w1s, w1_scales)
+        load_words(w1raw, w1_words)
+        load_x(2, 4)
+        load_x(4, 8)
+        nc.sync.dma_start(out=ut[:], in_=u.rearrange("(p r) c -> p r c", r=RT))
+        load_scales(w2s["x"], wx_scales)
+        load_scales(w2s["h"], wh_scales)
+        load_scales(w2s["v"], v1_scales)
+        load_words(w2["x"], wx_words)
+        load_words(w2["h"], wh_words)
+        load_words(w2["v"], v1_words)
+
+        free = list(range(8))
+        held = {}
+
+        def take(what, dtype=F32):
+            k = free.pop(0)
+            n = 512 if dtype == F32 else 1024
+            held[what] = (k, psum.tile([P, n], dtype, name="bank%d" % k))
+            return held[what][1]
+
+        def give(what):
+            k, tile = held[what]
+            free.append(k)
+            return tile
+
+        def spread_pe(g):
+            bank = take(("spread", g))
+            for t in range(4):
+                nc.tensor.transpose(
+                    bank[:, 128 * t : 128 * t + 128], xsc[:, 4 * g + t : 4 * g + t + 1].to_broadcast([P, P]), ident[:]
                 )
 
-        turn = [0]
+        def spread_s(g):
+            bank = give(("spread", g))
+            nc.scalar.copy(
+                out=sc[:, 512 * g : 512 * g + 512].rearrange("p (q t) -> p q t", t=4),
+                in_=bank[:].rearrange("p (t q) -> p q t", t=4),
+            )
 
-        def rotate():
-            turn[0] = (turn[0] + 1) % 8
-            return turn[0]
+        xb = {}
 
-        def bank_f32(k):
-            return psum.tile([P, 512], F32, name="bank%d" % k)
+        def product(r, c0=0, c1=D):
+            if c0 == 0:
+                xb[r] = keep.tile([P, D], BF16, align_bytes=64, name="xb%d" % r)
+            nc.vector.tensor_tensor(
+                out=xb[r][:, c0:c1], in0=xu[:, r, c0:c1].bitcast(FP8), in1=sc[:, c0:c1], op=ALU.mult
+            )
 
-        xT = {}
-
-        xbs = {}
-
-        def product(r):
-            xb = work.tile([P, D], BF16, align_bytes=64, name="xb")
-            n = 512 if r == 0 else 1024
-            for c in range(0, D, n):
-                nc.vector.tensor_tensor(
-                    out=xb[:, c : c + n], in0=xu[:, r, c : c + n].bitcast(FP8), in1=sc[:, c : c + n], op=ALU.mult
-                )
-            xbs[r] = xb
-
-        def turn_x(r):
-            words = xbs[r][:].bitcast(F32)
-            bank = bank_f32(rotate())
+        def turn(r):
+            words = xb[r][:].bitcast(F32)
+            bank = take(("x", r))
             for g in range(KG):
                 for w in range(2):
                     i = 2 * g + w
                     nc.tensor.transpose(
                         bank[:, 128 * i : 128 * i + 128], words[:, 256 * g + w : 256 * (g + 1) : 2], ident[:]
                     )
+
+        xT = {}
+
+        def copy_x(r):
+            bank = give(("x", r))
             if r % 2 == 0:
-                xT[r // 2] = work.tile([P, KG * 256 * 4], BF16, align_bytes=64, name="xTt")
+                xT[r // 2] = keep.tile([P, KG * 256 * 4], BF16, align_bytes=64, name="xT%d" % (r // 2))
             dst = xT[r // 2][:].bitcast(F32).rearrange("p (g n w) -> p g n w", g=KG, w=2)
             i = r % 2
             nc.scalar.copy(
@@ -150,42 +168,59 @@ def tile_grownetnewtontargets_w8_kernel(
                     out=xc[:, g, cols].bitcast(FP8X4), scales=xs[:, g, cols], in_=xT[pair][:, 1024 * g : 1024 * g + 1024]
                 )
 
-        def permute_w1(g):
-                nc.vector.tensor_copy(
-                    out=w1p[:, g, :].rearrange("p (c t m) -> p c t m", c=2, t=4),
-                    in_=w1raw[:, g, :].rearrange("p (c m t) -> p c t m", c=2, t=4),
-                )
+        def permute(g):
+            nc.vector.tensor_copy(
+                out=w1p[:, g, :].rearrange("p (c t m) -> p c t m", c=2, t=4),
+                in_=w1raw[:, g, :].rearrange("p (c m t) -> p c t m", c=2, t=4),
+            )
 
-        def permute_w1_scales():
+        def permute_scales():
             nc.vector.tensor_copy(
                 out=w1sp[:].rearrange("p (c t m) -> p c t m", c=2, t=4),
                 in_=w1s[:].rearrange("p (c m t) -> p c t m", c=2, t=4),
             )
 
-        def stage1(ci, j, on_vector=False):
-            c0, n = CHUNKS[ci]
-            bank = bank_f32(rotate())
+        def mm1(c, j):
+            bank = take(("z", c, j))
+            cols = slice(256 * c, 256 * c + 256)
             for g in range(KG):
                 nc.tensor.matmul_mx(
-                    out=bank[:, :n],
+                    out=bank[:, 0:256],
                     lhsT=w1p[:, g, 128 * j : 128 * j + 128].bitcast(FP8X4),
                     lhsT_scale=w1sp[4 * g : P, 128 * j : 128 * j + 128],
-                    rhs=xc[:, g, c0 : c0 + n].bitcast(FP8X4),
-                    rhs_scale=xs[:, g, c0 : c0 + n],
+                    rhs=xc[:, g, cols].bitcast(FP8X4),
+                    rhs_scale=xs[:, g, cols],
                     start=(g == 0),
                     stop=(g == KG - 1),
                 )
-            acc = sums[:, j, ci : ci + 1]
-            if on_vector:
-                nc.vector.tensor_scalar(
-                    out=r32[:, j, c0 : c0 + n], in0=bank[:, :n], scalar1=0.0, scalar2=None, op0=ALU.max, op1=ALU.add,
-                    accum_out=acc,
-                )
-            else:
-                nc.scalar.activation(out=r32[:, j, c0 : c0 + n], in_=bank[:, :n], func=ACT.Relu, accum_out=acc)
 
-        def means_early():
+        def relu_v(c, j):
+            bank = give(("z", c, j))
+            nc.vector.tensor_scalar(
+                out=r32[:, j, 256 * c : 256 * c + 256], in0=bank[:, 0:256], scalar1=0.0, scalar2=None, op0=ALU.max,
+                op1=ALU.add, accum_out=sums[:, j, c : c + 1],
+            )
+
+        def relu_s(c, j):
+            bank = give(("z", c, j))
+            nc.scalar.activation(
+                out=r32[:, j, 256 * c : 256 * c + 256], in_=bank[:, 0:256], func=ACT.Relu,
+                accum_out=sums[:, j, c : c + 1],
+            )
+
+        def gains():
+            nc.vector.tensor_copy(out=g1f[:], in_=g1b[:].rearrange("p g t -> p (g t)"))
+
+        def signs(k):
+            rs = slice(2 * k, 2 * k + 2)
+            nc.vector.tensor_scalar(
+                out=yh[:, rs, :], in0=ut[:, rs, :], scalar1=0.0, scalar2=0.5, op0=ALU.is_ge, op1=ALU.subtract
+            )
+
+        def early_sum():
             nc.vector.reduce_sum(out=part[:], in_=sums[:, :, 0:3], axis=AX.X)
+
+        def early_mean():
             nc.vector.tensor_scalar(out=part[:], in0=part[:], scalar1=1.0 / B, scalar2=None, op0=ALU.mult)
 
         def means(cg):
@@ -194,20 +229,32 @@ def tile_grownetnewtontargets_w8_kernel(
                 out=mean[:, js], in0=sums[:, js, 3], scalar=1.0 / B, in1=part[:, js], op0=ALU.mult, op1=ALU.add
             )
 
-        def centre(cg, half, ts=(0, 1, 2, 3)):
-            for t in ts:
-                j = 4 * cg + t
-                cols = slice(512 * half, 512 * half + 512)
-                nc.vector.tensor_scalar(
-                    out=hp[:, j, cols], in0=r32[:, j, cols], scalar1=mean[:, j : j + 1],
-                    scalar2=g1f[:, j : j + 1], op0=ALU.subtract, op1=ALU.mult,
-                )
+        def shifts(cg):
+            js = slice(4 * cg, 4 * cg + 4)
+            nc.vector.scalar_tensor_tensor(
+                out=shift[:, js], in0=mean[:, js], scalar=-1.0, in1=g1f[:, js], op0=ALU.mult, op1=ALU.mult
+            )
+
+        def centre_v(cg, h, t):
+            j = 4 * cg + t
+            cols = slice(512 * h, 512 * h + 512)
+            nc.vector.tensor_scalar(
+                out=hp[:, j, cols], in0=r32[:, j, cols], scalar1=mean[:, j : j + 1], scalar2=g1f[:, j : j + 1],
+                op0=ALU.subtract, op1=ALU.mult,
+            )
+
+        def centre_s(cg, h, t):
+            j = 4 * cg + t
+            cols = slice(512 * h, 512 * h + 512)
+            nc.scalar.activation(
+                out=hp[:, j, cols], in_=r32[:, j, cols], func=ACT.Identity, scale=g1f[:, j : j + 1],
+                bias=shift[:, j : j + 1],
+            )
 
         hi = {}
 
-        def inter(cg, blk, bk):
-            hi[cg, blk] = keep.tile([P, 1024], BF16, align_bytes=64, name="hi%d%d" % (cg, blk))
-            bank = psum.tile([P, 1024], BF16, name="bank%d" % bk)
+        def inter(cg, blk):
+            bank = take(("h", cg, blk), BF16)
             for k in range(2):
                 n0 = 256 * blk + 128 * k
                 nc.tensor.matmul(
@@ -217,61 +264,69 @@ def tile_grownetnewtontargets_w8_kernel(
                     start=True,
                     stop=True,
                 )
+
+        def copy_h(cg, blk):
+            bank = give(("h", cg, blk))
+            hi[cg, blk] = keep.tile([P, 1024], BF16, align_bytes=64, name="hi%d%d" % (cg, blk))
             nc.scalar.copy(out=hi[cg, blk][:], in_=bank[:])
 
         def quant_h(cg, blk):
-                cols = slice(256 * blk, 256 * blk + 256)
-                nc.vector.quantize_mx(out=hc[:, cg, cols].bitcast(FP8X4), scales=hs[:, cg, cols], in_=hi[cg, blk][:])
+            cols = slice(256 * blk, 256 * blk + 256)
+            nc.vector.quantize_mx(out=hc[:, cg, cols].bitcast(FP8X4), scales=hs[:, cg, cols], in_=hi[cg, blk][:])
 
-        pbank = {}
-        sbank = {}
-
-        def mm(bank, codes, scales, g, b, n, start, stop):
-            nc.tensor.matmul_mx(
-                out=bank[:],
-                lhsT=codes[:, g, 128 * b : 128 * b + 128].bitcast(FP8X4),
-                lhsT_scale=scales[:, g, 128 * b : 128 * b + 128],
-                rhs=w2[n][:, g, :].bitcast(FP8X4),
-                rhs_scale=w2s[n][4 * g : P, :],
-                start=start,
-                stop=stop,
-            )
+        def mm2(bank, codes, scales, b, n, first, last):
+            for g in range(KG):
+                nc.tensor.matmul_mx(
+                    out=bank[:],
+                    lhsT=codes[:, g, 128 * b : 128 * b + 128].bitcast(FP8X4),
+                    lhsT_scale=scales[:, g, 128 * b : 128 * b + 128],
+                    rhs=w2[n][:, g, :].bitcast(FP8X4),
+                    rhs_scale=w2s[n][4 * g : P, :],
+                    start=(first and g == 0),
+                    stop=(last and g == KG - 1),
+                )
 
         def px(b):
-            pbank[b] = bank_f32(b % 4)
-            for g in range(KG):
-                mm(pbank[b], xc, xs, g, b, "x", g == 0, False)
+            mm2(take(("p", b)), xc, xs, b, "x", True, False)
+
+        def wh(b):
+            mm2(held["p", b][1], hc, hs, b, "h", False, True)
+
+        def sv(b):
+            mm2(take(("s", b)), hc, hs, b, "v", True, True)
 
         th = {}
+        qq = {}
+        ww = {}
         ee = {}
 
-        def stage2(b, bk):
-            for g in range(KG):
-                mm(pbank[b], hc, hs, g, b, "h", False, g == KG - 1)
+        def tanh(b):
             th[b] = work.tile([P, C], F32, align_bytes=64, name="tht")
-            nc.scalar.activation(out=th[b][:], in_=pbank[b][:], func=ACT.Tanh)
-            sbank[b] = bank_f32(bk)
-            for g in range(KG):
-                mm(sbank[b], hc, hs, g, b, "v", g == 0, g == KG - 1)
+            nc.scalar.activation(out=th[b][:], in_=give(("p", b))[:], func=ACT.Tanh)
 
-        qq = {}
-
-        def epi_add(b, c0=0, c1=C):
+        def add(b, c0=0, c1=C):
             qq[b, c0] = work.tile([P, C], F32, align_bytes=64, name="qt")
+            bank = give(("s", b)) if c1 == C else held["s", b][1]
             nc.vector.tensor_tensor(
-                out=qq[b, c0][:, : c1 - c0], in0=sbank[b][:, c0:c1], in1=th[b][:, c0:c1], op=ALU.add
+                out=qq[b, c0][:, : c1 - c0], in0=bank[:, c0:c1], in1=th[b][:, c0:c1], op=ALU.add
             )
 
-        def epi_exp(b, c0=0, c1=C):
+        def mult(b, c0=0, c1=C):
+            ww[b, c0] = work.tile([P, C], F32, align_bytes=64, name="wt")
+            nc.vector.tensor_tensor(
+                out=ww[b, c0][:, : c1 - c0], in0=qq[b, c0][:, : c1 - c0], in1=yh[:, b, c0:c1], op=ALU.mult
+            )
+
+        def expo(b, c0=0, c1=C):
             n = c1 - c0
-            w = work.tile([P, C], F32, align_bytes=64, name="wt")
-            nc.vector.tensor_tensor(out=w[:, :n], in0=qq[b, c0][:, :n], in1=yh[:, b, c0:c1], op=ALU.mult)
             ee[b, c0] = work.tile([P, C], F32, align_bytes=64, name="et")
-            nc.scalar.activation(out=ee[b, c0][:, :n], in_=w[:, :n], func=ACT.Exp, scale=-1.6, bias=math.log(2.0))
+            nc.scalar.activation(
+                out=ee[b, c0][:, :n], in_=ww[b, c0][:, :n], func=ACT.Exp, scale=-1.6, bias=math.log(2.0)
+            )
 
         ov = out.rearrange("(p r) c -> p r c", r=RT)
 
-        def epi_out(b, c0=0, c1=C):
+        def finish(b, c0=0, c1=C):
             n = c1 - c0
             o = work.tile([P, C], F32, align_bytes=64, name="ot")
             nc.vector.scalar_tensor_tensor(
@@ -279,117 +334,222 @@ def tile_grownetnewtontargets_w8_kernel(
             )
             nc.sync.dma_start(out=ov[:, b, c0:c1], in_=o[:, :n])
 
-        def signs(r0, r1):
-            nc.vector.tensor_scalar(
-                out=yh[:, r0:r1, :], in0=ut[:, r0:r1, :], scalar1=0.0, scalar2=0.5, op0=ALU.is_ge, op1=ALU.subtract
-            )
-
-        product(0)
-        turn_x(0)
+        spread_pe(0)
+        spread_pe(1)
+        spread_s(0)
+        permute_scales()
+        spread_s(1)
+        product(0, 0, 512)
+        permute(0)
+        product(0, 512, D)
         product(1)
-        turn_x(1)
-        permute_w1_scales()
-        permute_w1(0)
-        quant_x(0)
-        permute_w1(1)
+        turn(0)
+        copy_x(0)
         product(2)
-        turn_x(2)
-        nc.vector.tensor_copy(out=g1f[:], in_=g1b[:].rearrange("p g t -> p (g t)"))
-        for j in range(3):
-            stage1(0, j)
+        turn(1)
+        copy_x(1)
         product(3)
-        turn_x(3)
-        for j in range(3, 6):
-            stage1(0, j)
+        turn(2)
+        copy_x(2)
+        quant_x(0)
+        turn(3)
+        permute(1)
+        copy_x(3)
         product(4)
+        mm1(0, 0)
+        mm1(0, 1)
+        relu_s(0, 0)
+        mm1(0, 2)
         quant_x(1)
-        turn_x(4)
-        for j in range(6, 8):
-            stage1(0, j)
-        for j in range(2):
-            stage1(1, j)
+        relu_s(0, 1)
+        mm1(0, 3)
+        relu_s(0, 2)
+        mm1(0, 4)
         product(5)
-        turn_x(5)
-        for j in range(2, 5):
-            stage1(1, j)
+        mm1(0, 5)
+        relu_s(0, 3)
+        mm1(0, 6)
+        relu_s(0, 4)
+        mm1(0, 7)
+        relu_s(0, 5)
+        mm1(1, 0)
+        relu_s(0, 6)
         product(6)
-        quant_x(2)
-        turn_x(6)
-        for j in range(5, 8):
-            stage1(1, j)
+        mm1(1, 1)
+        relu_s(0, 7)
+        mm1(1, 2)
+        mm1(1, 6)
+        turn(4)
         product(7)
-        turn_x(7)
-        for j in range(6):
-            stage1(2, j)
-        signs(0, 8)
+        turn(5)
+        copy_x(4)
+        turn(6)
+        relu_v(1, 6)
+        copy_x(5)
+        gains()
+        turn(7)
+        relu_s(1, 0)
+        quant_x(2)
+        mm1(1, 3)
+        copy_x(6)
+        mm1(1, 4)
+        relu_s(1, 1)
+        mm1(1, 5)
+        copy_x(7)
+        mm1(1, 7)
+        mm1(2, 0)
+        relu_v(1, 7)
+        relu_s(1, 2)
+        mm1(2, 1)
+        relu_s(1, 3)
         quant_x(3)
-        stage1(2, 6, True)
-        stage1(2, 7, True)
-        means_early()
-        for j in range(4):
-            stage1(3, j)
-            stage1(3, 4 + j, True)
-        for b in range(4):
-            px(b)
+        mm1(2, 2)
+        mm1(2, 6)
+        relu_s(1, 4)
+        mm1(2, 3)
+        relu_s(1, 5)
+        relu_v(2, 6)
+        mm1(2, 4)
+        relu_s(2, 0)
+        mm1(2, 5)
+        relu_s(2, 1)
+        mm1(2, 7)
+        relu_s(2, 2)
+        mm1(3, 0)
+        relu_v(2, 7)
+        relu_s(2, 3)
+        mm1(3, 4)
+        relu_s(2, 4)
+        mm1(3, 1)
+        relu_v(3, 4)
+        mm1(3, 5)
+        relu_s(2, 5)
+        mm1(3, 2)
+        relu_s(3, 0)
+        early_sum()
+        relu_v(3, 5)
+        mm1(3, 6)
+        relu_s(3, 1)
+        mm1(3, 3)
+        early_mean()
+        relu_s(3, 2)
+        relu_v(3, 6)
+        mm1(3, 7)
+        relu_s(3, 3)
+        px(0)
         means(0)
+        shifts(0)
+        relu_v(3, 7)
+        px(1)
+        centre_s(0, 0, 3)
+        centre_v(0, 0, 0)
+        centre_v(0, 0, 1)
+        px(2)
         means(1)
-        centre(0, 0)
-        inter(0, 0, 4)
-        inter(0, 1, 5)
-        centre(1, 0)
-        inter(1, 0, 6)
-        inter(1, 1, 7)
-        centre(0, 1, (0, 1))
+        shifts(1)
+        centre_v(0, 0, 2)
+        centre_s(1, 0, 3)
+        px(3)
+        centre_v(1, 0, 0)
+        centre_v(1, 0, 1)
+        centre_s(0, 1, 3)
+        inter(0, 0)
+        centre_v(1, 0, 2)
+        centre_v(0, 1, 0)
+        inter(0, 1)
+        signs(0)
+        copy_h(0, 0)
+        signs(1)
+        inter(1, 0)
+        centre_v(0, 1, 1)
+        copy_h(0, 1)
+        centre_v(0, 1, 2)
+        inter(1, 1)
+        centre_v(1, 1, 0)
+        copy_h(1, 0)
         quant_h(0, 0)
-        centre(0, 1, (2, 3))
+        inter(0, 2)
+        centre_v(1, 1, 1)
+        copy_h(1, 1)
         quant_h(1, 0)
-        centre(1, 1)
+        inter(0, 3)
         quant_h(0, 1)
+        copy_h(0, 2)
         quant_h(1, 1)
-        stage2(0, 4)
-        stage2(1, 5)
-        inter(0, 2, 6)
-        inter(1, 2, 7)
-        epi_add(0)
-        epi_add(1)
-        epi_exp(0)
-        epi_exp(1)
-        inter(0, 3, 4)
-        inter(1, 3, 5)
+        wh(0)
+        centre_v(1, 1, 2)
         quant_h(0, 2)
+        sv(0)
+        tanh(0)
+        signs(2)
+        signs(3)
+        wh(1)
+        centre_s(1, 1, 3)
+        add(0)
+        sv(1)
+        tanh(1)
+        mult(0)
+        wh(2)
+        copy_h(0, 3)
+        add(1)
+        inter(1, 2)
+        expo(0)
+        inter(1, 3)
+        mult(1)
+        copy_h(1, 2)
+        sv(2)
+        finish(0)
+        tanh(2)
+        wh(3)
         quant_h(1, 2)
-        stage2(2, 6)
-        stage2(3, 7)
-        epi_out(0)
-        quant_h(0, 3)
-        epi_out(1)
-        quant_h(1, 3)
+        expo(1)
+        add(2)
         px(4)
-        stage2(4, 4)
+        tanh(3)
+        finish(1)
+        sv(3)
+        copy_h(1, 3)
+        mult(2)
+        wh(4)
+        quant_h(0, 3)
+        sv(4)
+        add(3)
+        tanh(4)
         px(5)
-        stage2(5, 5)
-        epi_add(2)
-        epi_add(3)
-        epi_exp(2)
-        epi_exp(3)
+        quant_h(1, 3)
+        expo(2)
+        add(4)
+        wh(5)
+        finish(2)
+        sv(5)
+        tanh(5)
+        mult(3)
         px(6)
-        stage2(6, 6)
+        mult(4)
+        wh(6)
+        expo(3)
+        add(5)
+        sv(6)
+        expo(4)
+        finish(3)
         px(7)
-        stage2(7, 7)
-        epi_add(4)
-        epi_out(2)
-        epi_exp(4)
-        epi_add(5)
-        epi_out(3)
-        epi_exp(5)
-        epi_add(6)
-        epi_out(4)
-        epi_exp(6)
-        epi_add(7, 0, 256)
-        epi_add(7, 256, 512)
-        epi_exp(7, 0, 256)
-        epi_exp(7, 256, 512)
-        epi_out(5)
-        epi_out(6)
-        epi_out(7, 0, 256)
-        epi_out(7, 256, 512)
+        tanh(6)
+        mult(5)
+        wh(7)
+        finish(4)
+        sv(7)
+        expo(5)
+        add(6)
+        tanh(7)
+        finish(5)
+        mult(6)
+        add(7, 0, HALF)
+        expo(6)
+        add(7, HALF, C)
+        mult(7, 0, HALF)
+        mult(7, HALF, C)
+        expo(7, 0, HALF)
+        finish(6)
+        expo(7, HALF, C)
+        finish(7, 0, HALF)
+        finish(7, HALF, C)

@@ -50,7 +50,6 @@ def tile_grownetnewtontargets_w8_kernel(
         ut = keep.tile([P, RT, C], BF16, align_bytes=64)
         yh = keep.tile([P, RT, C], BF16, align_bytes=64)
         ident = keep.tile([P, P], F32, align_bytes=64)
-        identb = keep.tile([P, P], BF16, align_bytes=64)
         dummy = keep.tile([P, 1], F32, align_bytes=64)
         dummy2 = keep.tile([P, 1], F32, align_bytes=64)
         xc = keep.tile([P, KG, B], U32, align_bytes=64)
@@ -69,7 +68,6 @@ def tile_grownetnewtontargets_w8_kernel(
         nc.scalar.dma_start(out=xsc[:], in_=x_scale.rearrange("o (g p t) -> p (o g) t", g=KG, t=4))
         nc.scalar.activation(out=dummy2[:], in_=dummy[:], func=ACT.Exp)
         nc.vector.memset(w1s[:].bitcast(I32), 0)
-        make_identity(nc, identb[:])
         for n in ("x", "h", "v"):
             nc.vector.memset(w2s[n][:].bitcast(I32), 0)
         nc.scalar.dma_start(out=g1b[:], in_=g1.rearrange("(g p t) -> p g t", g=KG, t=4))
@@ -169,16 +167,18 @@ def tile_grownetnewtontargets_w8_kernel(
                 )
 
         def permute(g):
-            nc.vector.tensor_copy(
-                out=w1p[:, g, :].rearrange("p (c t m) -> p c t m", c=2, t=4),
-                in_=w1raw[:, g, :].rearrange("p (c m t) -> p c t m", c=2, t=4),
-            )
+            for c in range(0, H, 512):
+                nc.vector.tensor_copy(
+                    out=w1p[:, g, c : c + 512].rearrange("p (t b i) -> p b t i", t=4, i=4),
+                    in_=w1raw[:, g, c : c + 512].rearrange("p (b i t) -> p b t i", t=4, i=4),
+                )
 
         def permute_scales():
-            nc.vector.tensor_copy(
-                out=w1sp[:].rearrange("p (c t m) -> p c t m", c=2, t=4),
-                in_=w1s[:].rearrange("p (c m t) -> p c t m", c=2, t=4),
-            )
+            for c in range(0, H, 512):
+                nc.vector.tensor_copy(
+                    out=w1sp[:, c : c + 512].rearrange("p (t b i) -> p b t i", t=4, i=16),
+                    in_=w1s[:, c : c + 512].rearrange("p (b i t) -> p b t i", t=4, i=16),
+                )
 
         def mm1(c, j):
             bank = take(("z", c, j))
@@ -253,22 +253,19 @@ def tile_grownetnewtontargets_w8_kernel(
 
         hi = {}
 
-        def inter(cg, blk):
-            bank = take(("h", cg, blk), BF16)
-            for k in range(2):
-                n0 = 256 * blk + 128 * k
-                nc.tensor.matmul(
-                    out=bank[:, 512 * k : 512 * k + 512].rearrange("p (n t) -> p n t", t=4),
-                    lhsT=identb[:],
-                    rhs=hp[:, 4 * cg : 4 * cg + 4, n0 : n0 + 128].rearrange("p t n -> p n t"),
-                    start=True,
-                    stop=True,
-                )
-
-        def copy_h(cg, blk):
-            bank = give(("h", cg, blk))
+        def weave(cg, blk):
             hi[cg, blk] = keep.tile([P, 1024], BF16, align_bytes=64, name="hi%d%d" % (cg, blk))
-            nc.scalar.copy(out=hi[cg, blk][:], in_=bank[:])
+            dst = hi[cg, blk][:].rearrange("p (c i t) -> p c t i", i=4, t=4)
+            src = hp[:, 4 * cg : 4 * cg + 4, 256 * blk : 256 * blk + 256].rearrange("p t (c i) -> p c t i", i=4)
+            return dst, src
+
+        def weave_v(cg, blk):
+            dst, src = weave(cg, blk)
+            nc.vector.tensor_copy(out=dst, in_=src)
+
+        def weave_s(cg, blk):
+            dst, src = weave(cg, blk)
+            nc.scalar.copy(out=dst, in_=src)
 
         def quant_h(cg, blk):
             cols = slice(256 * blk, 256 * blk + 256)
@@ -378,177 +375,169 @@ def tile_grownetnewtontargets_w8_kernel(
         mm1(1, 1)
         relu_s(0, 7)
         mm1(1, 2)
-        mm1(1, 6)
-        turn(4)
-        product(7)
-        turn(5)
-        copy_x(4)
-        turn(6)
-        relu_v(1, 6)
-        copy_x(5)
-        gains()
-        turn(7)
         relu_s(1, 0)
-        quant_x(2)
         mm1(1, 3)
-        copy_x(6)
         mm1(1, 4)
         relu_s(1, 1)
+        product(7)
+        turn(4)
+        relu_s(1, 2)
+        relu_s(1, 3)
+        turn(5)
+        copy_x(4)
+        gains()
+        turn(6)
+        copy_x(5)
+        turn(7)
+        relu_s(1, 4)
+        quant_x(2)
         mm1(1, 5)
+        copy_x(6)
+        signs(0)
+        mm1(1, 6)
         copy_x(7)
         mm1(1, 7)
         mm1(2, 0)
+        relu_s(1, 5)
         relu_v(1, 7)
-        relu_s(1, 2)
         mm1(2, 1)
-        relu_s(1, 3)
+        relu_s(1, 6)
         quant_x(3)
         mm1(2, 2)
-        mm1(2, 6)
-        relu_s(1, 4)
-        mm1(2, 3)
-        relu_s(1, 5)
-        relu_v(2, 6)
-        mm1(2, 4)
         relu_s(2, 0)
-        mm1(2, 5)
+        mm1(2, 3)
+        mm1(2, 4)
         relu_s(2, 1)
-        mm1(2, 7)
+        mm1(2, 5)
         relu_s(2, 2)
-        mm1(3, 0)
-        relu_v(2, 7)
+        mm1(2, 6)
         relu_s(2, 3)
-        mm1(3, 4)
+        mm1(2, 7)
         relu_s(2, 4)
-        mm1(3, 1)
-        relu_v(3, 4)
-        mm1(3, 5)
+        mm1(3, 0)
         relu_s(2, 5)
-        mm1(3, 2)
+        relu_v(2, 7)
+        mm1(3, 1)
+        relu_s(2, 6)
+        mm1(3, 5)
         relu_s(3, 0)
+        mm1(3, 2)
         early_sum()
         relu_v(3, 5)
-        mm1(3, 6)
-        relu_s(3, 1)
         mm1(3, 3)
+        relu_s(3, 1)
         early_mean()
+        mm1(3, 6)
+        signs(1)
         relu_s(3, 2)
+        mm1(3, 4)
+        relu_s(3, 3)
         relu_v(3, 6)
         mm1(3, 7)
-        relu_s(3, 3)
-        px(0)
+        relu_s(3, 4)
         means(0)
         shifts(0)
+        px(0)
         relu_v(3, 7)
-        px(1)
         centre_s(0, 0, 3)
         centre_v(0, 0, 0)
-        centre_v(0, 0, 1)
-        px(2)
+        px(1)
         means(1)
         shifts(1)
-        centre_v(0, 0, 2)
+        centre_v(0, 0, 1)
+        px(2)
         centre_s(1, 0, 3)
-        px(3)
+        centre_v(0, 0, 2)
         centre_v(1, 0, 0)
+        px(3)
+        weave_s(0, 1)
         centre_v(1, 0, 1)
-        centre_s(0, 1, 3)
-        inter(0, 0)
         centre_v(1, 0, 2)
-        centre_v(0, 1, 0)
-        inter(0, 1)
-        signs(0)
-        copy_h(0, 0)
-        signs(1)
-        inter(1, 0)
-        centre_v(0, 1, 1)
-        copy_h(0, 1)
-        centre_v(0, 1, 2)
-        inter(1, 1)
-        centre_v(1, 1, 0)
-        copy_h(1, 0)
+        px(4)
+        weave_v(0, 0)
+        px(5)
+        centre_s(0, 1, 3)
+        weave_v(1, 0)
+        centre_s(1, 1, 3)
         quant_h(0, 0)
-        inter(0, 2)
-        centre_v(1, 1, 1)
-        copy_h(1, 1)
         quant_h(1, 0)
-        inter(0, 3)
-        quant_h(0, 1)
-        copy_h(0, 2)
-        quant_h(1, 1)
+        weave_s(1, 1)
+        centre_v(0, 1, 0)
         wh(0)
-        centre_v(1, 1, 2)
-        quant_h(0, 2)
+        centre_v(0, 1, 1)
+        centre_v(0, 1, 2)
         sv(0)
+        quant_h(0, 1)
         tanh(0)
         signs(2)
-        signs(3)
         wh(1)
-        centre_s(1, 1, 3)
+        quant_h(1, 1)
+        weave_s(0, 2)
         add(0)
         sv(1)
-        tanh(1)
-        mult(0)
+        centre_v(1, 1, 0)
         wh(2)
-        copy_h(0, 3)
-        add(1)
-        inter(1, 2)
-        expo(0)
-        inter(1, 3)
-        mult(1)
-        copy_h(1, 2)
+        mult(0)
+        tanh(1)
         sv(2)
-        finish(0)
-        tanh(2)
+        centre_v(1, 1, 1)
+        expo(0)
+        centre_v(1, 1, 2)
         wh(3)
-        quant_h(1, 2)
-        expo(1)
-        add(2)
-        px(4)
-        tanh(3)
-        finish(1)
+        quant_h(0, 2)
+        tanh(2)
+        add(1)
         sv(3)
-        copy_h(1, 3)
-        mult(2)
+        weave_s(1, 2)
+        signs(3)
+        mult(1)
+        add(2)
+        expo(1)
+        quant_h(1, 2)
+        tanh(3)
+        finish(0)
         wh(4)
-        quant_h(0, 3)
-        sv(4)
+        weave_s(0, 3)
+        mult(2)
+        px(6)
         add(3)
-        tanh(4)
-        px(5)
-        quant_h(1, 3)
+        sv(4)
+        finish(1)
         expo(2)
-        add(4)
+        px(7)
+        mult(3)
+        tanh(4)
         wh(5)
         finish(2)
+        weave_s(1, 3)
         sv(5)
+        add(4)
+        quant_h(0, 3)
         tanh(5)
-        mult(3)
-        px(6)
+        quant_h(1, 3)
         mult(4)
-        wh(6)
         expo(3)
+        wh(6)
         add(5)
         sv(6)
         expo(4)
         finish(3)
-        px(7)
-        tanh(6)
-        mult(5)
         wh(7)
+        tanh(6)
         finish(4)
         sv(7)
-        expo(5)
-        add(6)
         tanh(7)
-        finish(5)
+        add(6)
+        mult(5)
         mult(6)
+        expo(5)
         add(7, 0, HALF)
         expo(6)
         add(7, HALF, C)
         mult(7, 0, HALF)
-        mult(7, HALF, C)
+        finish(5)
         expo(7, 0, HALF)
+        mult(7, HALF, C)
         finish(6)
         expo(7, HALF, C)
         finish(7, 0, HALF)

@@ -314,6 +314,10 @@ def tile_grownetnewtontargets_w8_kernel(
                 out=ww[b, c0][:, : c1 - c0], in0=qq[b, c0][:, : c1 - c0], in1=yh[:, b, c0:c1], op=ALU.mult
             )
 
+        def mult_g(b):
+            ww[b, 0] = work.tile([P, C], F32, align_bytes=64, name="wt")
+            nc.gpsimd.tensor_tensor(out=ww[b, 0][:], in0=qq[b, 0][:], in1=yh[:, b, :], op=ALU.mult)
+
         def expo(b, c0=0, c1=C):
             n = c1 - c0
             ee[b, c0] = work.tile([P, C], F32, align_bytes=64, name="et")
@@ -337,81 +341,81 @@ def tile_grownetnewtontargets_w8_kernel(
         permute_scales()
         spread_s(1)
         product(0, 0, 512)
-        permute(0)
         product(0, 512, D)
         product(1)
         turn(0)
         copy_x(0)
-        product(2)
+        permute(0)
         turn(1)
-        copy_x(1)
-        product(3)
-        turn(2)
-        copy_x(2)
-        quant_x(0)
-        turn(3)
         permute(1)
-        copy_x(3)
-        product(4)
+        copy_x(1)
+        quant_x(0)
+        product(2)
         mm1(0, 0)
         mm1(0, 1)
         relu_s(0, 0)
         mm1(0, 2)
-        quant_x(1)
+        product(3)
         relu_s(0, 1)
         mm1(0, 3)
-        relu_s(0, 2)
         mm1(0, 4)
-        product(5)
+        relu_s(0, 2)
         mm1(0, 5)
         relu_s(0, 3)
-        mm1(0, 6)
+        turn(2)
         relu_s(0, 4)
-        mm1(0, 7)
+        product(4)
         relu_s(0, 5)
-        mm1(1, 0)
-        relu_s(0, 6)
-        product(6)
-        mm1(1, 1)
-        relu_s(0, 7)
-        mm1(1, 2)
-        relu_s(1, 0)
-        mm1(1, 3)
-        mm1(1, 4)
-        relu_s(1, 1)
-        product(7)
+        turn(3)
+        copy_x(2)
+        mm1(0, 6)
+        product(5)
+        copy_x(3)
+        mm1(0, 7)
         turn(4)
-        relu_s(1, 2)
-        relu_s(1, 3)
+        relu_s(0, 6)
+        relu_s(0, 7)
+        quant_x(1)
         turn(5)
         copy_x(4)
-        gains()
-        turn(6)
+        product(6)
+        mm1(1, 0)
         copy_x(5)
-        turn(7)
-        relu_s(1, 4)
-        quant_x(2)
+        mm1(1, 1)
+        relu_s(1, 0)
+        mm1(1, 2)
+        gains()
+        mm1(1, 3)
+        product(7)
+        relu_s(1, 1)
+        mm1(1, 4)
+        relu_s(1, 2)
         mm1(1, 5)
-        copy_x(6)
-        signs(0)
+        relu_s(1, 3)
         mm1(1, 6)
-        copy_x(7)
+        relu_s(1, 4)
+        turn(6)
+        signs(0)
+        relu_s(1, 5)
+        quant_x(2)
+        turn(7)
+        relu_s(1, 6)
+        copy_x(6)
         mm1(1, 7)
         mm1(2, 0)
-        relu_s(1, 5)
+        copy_x(7)
         relu_v(1, 7)
         mm1(2, 1)
-        relu_s(1, 6)
-        quant_x(3)
         mm1(2, 2)
         relu_s(2, 0)
+        quant_x(3)
         mm1(2, 3)
-        mm1(2, 4)
         relu_s(2, 1)
-        mm1(2, 5)
+        mm1(2, 4)
         relu_s(2, 2)
-        mm1(2, 6)
+        mm1(2, 5)
         relu_s(2, 3)
+        mm1(2, 6)
         mm1(2, 7)
         relu_s(2, 4)
         mm1(3, 0)
@@ -420,121 +424,121 @@ def tile_grownetnewtontargets_w8_kernel(
         mm1(3, 1)
         relu_s(2, 6)
         mm1(3, 5)
+        signs(1)
         relu_s(3, 0)
         mm1(3, 2)
         early_sum()
-        relu_v(3, 5)
         mm1(3, 3)
         relu_s(3, 1)
         early_mean()
+        relu_v(3, 5)
         mm1(3, 6)
-        signs(1)
         relu_s(3, 2)
         mm1(3, 4)
         relu_s(3, 3)
         relu_v(3, 6)
         mm1(3, 7)
         relu_s(3, 4)
-        means(0)
-        shifts(0)
         px(0)
+        means(0)
         relu_v(3, 7)
-        centre_s(0, 0, 3)
-        centre_v(0, 0, 0)
         px(1)
+        shifts(0)
+        centre_v(0, 0, 0)
+        centre_s(0, 0, 3)
         means(1)
-        shifts(1)
         centre_v(0, 0, 1)
         px(2)
-        centre_s(1, 0, 3)
+        shifts(1)
         centre_v(0, 0, 2)
-        centre_v(1, 0, 0)
         px(3)
-        weave_s(0, 1)
+        centre_s(1, 0, 3)
+        centre_v(1, 0, 0)
         centre_v(1, 0, 1)
-        centre_v(1, 0, 2)
         px(4)
+        weave_s(0, 1)
+        centre_v(1, 0, 2)
         weave_v(0, 0)
-        px(5)
-        centre_s(0, 1, 3)
         weave_v(1, 0)
-        centre_s(1, 1, 3)
+        weave_s(1, 1)
         quant_h(0, 0)
         quant_h(1, 0)
-        weave_s(1, 1)
+        centre_s(0, 1, 3)
         centre_v(0, 1, 0)
         wh(0)
         centre_v(0, 1, 1)
+        centre_s(1, 1, 3)
         centre_v(0, 1, 2)
         sv(0)
         quant_h(0, 1)
         tanh(0)
-        signs(2)
-        wh(1)
         quant_h(1, 1)
-        weave_s(0, 2)
-        add(0)
-        sv(1)
+        wh(1)
         centre_v(1, 1, 0)
+        weave_s(0, 2)
+        sv(1)
+        signs(2)
+        centre_v(1, 1, 1)
         wh(2)
-        mult(0)
+        centre_v(1, 1, 2)
+        add(0)
         tanh(1)
         sv(2)
-        centre_v(1, 1, 1)
-        expo(0)
-        centre_v(1, 1, 2)
-        wh(3)
         quant_h(0, 2)
-        tanh(2)
-        add(1)
-        sv(3)
+        wh(3)
         weave_s(1, 2)
-        signs(3)
-        mult(1)
-        add(2)
-        expo(1)
+        mult(0)
+        sv(3)
+        add(1)
+        tanh(2)
         quant_h(1, 2)
+        signs(3)
         tanh(3)
-        finish(0)
         wh(4)
-        weave_s(0, 3)
-        mult(2)
-        px(6)
-        add(3)
+        add(2)
+        mult_g(1)
+        expo(0)
         sv(4)
-        finish(1)
-        expo(2)
+        add(3)
+        weave_s(0, 3)
+        px(5)
+        finish(0)
+        px(6)
+        mult(2)
         px(7)
-        mult(3)
         tanh(4)
+        mult_g(3)
         wh(5)
-        finish(2)
         weave_s(1, 3)
-        sv(5)
         add(4)
-        quant_h(0, 3)
-        tanh(5)
-        quant_h(1, 3)
+        sv(5)
         mult(4)
-        expo(3)
+        expo(1)
+        quant_h(0, 3)
+        quant_h(1, 3)
+        expo(2)
+        finish(1)
         wh(6)
-        add(5)
+        tanh(5)
+        finish(2)
         sv(6)
+        expo(3)
+        add(5)
+        wh(7)
         expo(4)
         finish(3)
-        wh(7)
+        sv(7)
         tanh(6)
         finish(4)
-        sv(7)
         tanh(7)
         add(6)
-        mult(5)
+        mult_g(5)
+        add(7, 0, HALF)
+        add(7, HALF, C)
         mult(6)
         expo(5)
-        add(7, 0, HALF)
-        expo(6)
-        add(7, HALF, C)
         mult(7, 0, HALF)
+        expo(6)
         finish(5)
         expo(7, 0, HALF)
         mult(7, HALF, C)

import math
from contextlib import ExitStack

import concourse.mybir as mybir
from concourse.masks import make_identity

F32 = mybir.dt.float32
BF16 = mybir.dt.bfloat16
I32 = mybir.dt.int32
U32 = mybir.dt.uint32
U8 = mybir.dt.uint8
FP8 = mybir.dt.float8_e4m3fn
FP8X4 = mybir.dt.float8_e4m3fn_x4
ALU = mybir.AluOpType
ACT = mybir.ActivationFunctionType
AX = mybir.AxisListType

P = 128
B, D, H, C = 1024, 1024, 1024, 512
RT = B // P
KG = D // 512
FLOPS = 2 * B * D * H + 3 * 2 * B * H * C
HALF = C // 2


def tile_grownetnewtontargets_w8_kernel(
    tc, x_bytes, x_scale, w1_words, w1_scales, g1, v1_words, v1_scales, wx_words, wx_scales, wh_words, wh_scales, u, out
):
    nc = tc.nc
    with ExitStack() as ctx:
        keep = ctx.enter_context(tc.tile_pool(name="keep", bufs=1))
        work = ctx.enter_context(tc.tile_pool(name="work", bufs=4))
        psum = ctx.enter_context(tc.psum_pool(name="psum", bufs=1))
        ctx.enter_context(tc.manual_schedule())

        xu = keep.tile([P, RT, D], U8, align_bytes=64)
        xsc = keep.tile([P, KG * 4], F32, align_bytes=64)
        sc = keep.tile([P, D], F32, align_bytes=64)
        w1raw = keep.tile([P, KG, H], I32, align_bytes=64)
        w1p = keep.tile([P, KG, H], I32, align_bytes=64)
        w1s = keep.tile([P, H], U8, align_bytes=64)
        w1sp = keep.tile([P, H], U8, align_bytes=64)
        w2 = {}
        w2s = {}
        for n in ("x", "h", "v"):
            w2[n] = keep.tile([P, KG, C], I32, align_bytes=64, name="w2" + n)
            w2s[n] = keep.tile([P, C], U8, align_bytes=64, name="w2s" + n)
        g1b = keep.tile([P, KG, 4], BF16, align_bytes=64)
        g1f = keep.tile([P, KG * 4], F32, align_bytes=64)
        ut = keep.tile([P, RT, C], BF16, align_bytes=64)
        yh = keep.tile([P, RT, C], BF16, align_bytes=64)
        ident = keep.tile([P, P], F32, align_bytes=64)
        dummy = keep.tile([P, 1], F32, align_bytes=64)
        dummy2 = keep.tile([P, 1], F32, align_bytes=64)
        xc = keep.tile([P, KG, B], U32, align_bytes=64)
        xs = keep.tile([P, KG, B], U8, align_bytes=64)
        r32 = keep.tile([P, 8, B], F32, align_bytes=64)
        hp = keep.tile([P, 8, B], BF16, align_bytes=64)
        sums = keep.tile([P, 8, 4], F32, align_bytes=64)
        part = keep.tile([P, 8], F32, align_bytes=64)
        mean = keep.tile([P, 8], F32, align_bytes=64)
        shift = keep.tile([P, 8], F32, align_bytes=64)
        hc = keep.tile([P, KG, B], U32, align_bytes=64)
        hs = keep.tile([P, KG, B], U8, align_bytes=64)

        make_identity(nc, ident[:])
        nc.vector.memset(dummy[:], 0.0)
        nc.scalar.dma_start(out=xsc[:], in_=x_scale.rearrange("o (g p t) -> p (o g) t", g=KG, t=4))
        nc.scalar.activation(out=dummy2[:], in_=dummy[:], func=ACT.Exp)
        nc.vector.memset(w1s[:].bitcast(I32), 0)
        for n in ("x", "h", "v"):
            nc.vector.memset(w2s[n][:].bitcast(I32), 0)
        nc.scalar.dma_start(out=g1b[:], in_=g1.rearrange("(g p t) -> p g t", g=KG, t=4))

        xv = x_bytes.rearrange("(p r) k -> p r k", r=RT)

        def load_x(r0, r1):
            nc.sync.dma_start(out=xu[:, r0:r1, :], in_=xv[:, r0:r1, :])

        def load_scales(tile, scales):
            for q in range(4):
                nc.sync.dma_start(
                    out=tile[32 * q : 32 * q + 8, :].bitcast(I32), in_=scales[:, 4 * q : 4 * q + 4, :].bitcast(I32)
                )

        def load_words(tile, words):
            for g in range(KG):
                nc.sync.dma_start(out=tile[:, g, :], in_=words[g].rearrange("p n t -> p (n t)").bitcast(I32))

        load_x(0, 2)
        load_scales(w1s, w1_scales)
        load_words(w1raw, w1_words)
        load_x(2, 4)
        load_x(4, 8)
        nc.sync.dma_start(out=ut[:], in_=u.rearrange("(p r) c -> p r c", r=RT))
        load_scales(w2s["x"], wx_scales)
        load_scales(w2s["h"], wh_scales)
        load_scales(w2s["v"], v1_scales)
        load_words(w2["x"], wx_words)
        load_words(w2["h"], wh_words)
        load_words(w2["v"], v1_words)

        free = list(range(8))
        held = {}

        def take(what, dtype=F32):
            k = free.pop(0)
            n = 512 if dtype == F32 else 1024
            held[what] = (k, psum.tile([P, n], dtype, name="bank%d" % k))
            return held[what][1]

        def give(what):
            k, tile = held[what]
            free.append(k)
            return tile

        def spread_pe(g):
            bank = take(("spread", g))
            for t in range(4):
                nc.tensor.transpose(
                    bank[:, 128 * t : 128 * t + 128], xsc[:, 4 * g + t : 4 * g + t + 1].to_broadcast([P, P]), ident[:]
                )

        def spread_s(g):
            bank = give(("spread", g))
            nc.scalar.copy(
                out=sc[:, 512 * g : 512 * g + 512].rearrange("p (q t) -> p q t", t=4),
                in_=bank[:].rearrange("p (t q) -> p q t", t=4),
            )

        xb = {}

        def product(r, c0=0, c1=D):
            if c0 == 0:
                xb[r] = keep.tile([P, D], BF16, align_bytes=64, name="xb%d" % r)
            nc.vector.tensor_tensor(
                out=xb[r][:, c0:c1], in0=xu[:, r, c0:c1].bitcast(FP8), in1=sc[:, c0:c1], op=ALU.mult
            )

        def turn(r):
            words = xb[r][:].bitcast(F32)
            bank = take(("x", r))
            for g in range(KG):
                for w in range(2):
                    i = 2 * g + w
                    nc.tensor.transpose(
                        bank[:, 128 * i : 128 * i + 128], words[:, 256 * g + w : 256 * (g + 1) : 2], ident[:]
                    )

        xT = {}

        def copy_x(r):
            bank = give(("x", r))
            if r % 2 == 0:
                xT[r // 2] = keep.tile([P, KG * 256 * 4], BF16, align_bytes=64, name="xT%d" % (r // 2))
            dst = xT[r // 2][:].bitcast(F32).rearrange("p (g n w) -> p g n w", g=KG, w=2)
            i = r % 2
            nc.scalar.copy(
                out=dst[:, :, 128 * i : 128 * i + 128, :], in_=bank[:].rearrange("p (g w n) -> p g n w", g=KG, w=2)
            )

        def quant_x(pair):
            for g in range(KG):
                cols = slice(256 * pair, 256 * pair + 256)
                nc.vector.quantize_mx(
                    out=xc[:, g, cols].bitcast(FP8X4), scales=xs[:, g, cols], in_=xT[pair][:, 1024 * g : 1024 * g + 1024]
                )

        def permute(g):
            for c in range(0, H, 512):
                nc.vector.tensor_copy(
                    out=w1p[:, g, c : c + 512].rearrange("p (t b i) -> p b t i", t=4, i=4),
                    in_=w1raw[:, g, c : c + 512].rearrange("p (b i t) -> p b t i", t=4, i=4),
                )

        def permute_scales():
            for c in range(0, H, 512):
                nc.vector.tensor_copy(
                    out=w1sp[:, c : c + 512].rearrange("p (t b i) -> p b t i", t=4, i=16),
                    in_=w1s[:, c : c + 512].rearrange("p (b i t) -> p b t i", t=4, i=16),
                )

        def mm1(c, j):
            bank = take(("z", c, j))
            cols = slice(256 * c, 256 * c + 256)
            for g in range(KG):
                nc.tensor.matmul_mx(
                    out=bank[:, 0:256],
                    lhsT=w1p[:, g, 128 * j : 128 * j + 128].bitcast(FP8X4),
                    lhsT_scale=w1sp[4 * g : P, 128 * j : 128 * j + 128],
                    rhs=xc[:, g, cols].bitcast(FP8X4),
                    rhs_scale=xs[:, g, cols],
                    start=(g == 0),
                    stop=(g == KG - 1),
                )

        def relu_v(c, j):
            bank = give(("z", c, j))
            nc.vector.tensor_scalar(
                out=r32[:, j, 256 * c : 256 * c + 256], in0=bank[:, 0:256], scalar1=0.0, scalar2=None, op0=ALU.max,
                op1=ALU.add, accum_out=sums[:, j, c : c + 1],
            )

        def relu_s(c, j):
            bank = give(("z", c, j))
            nc.scalar.activation(
                out=r32[:, j, 256 * c : 256 * c + 256], in_=bank[:, 0:256], func=ACT.Relu,
                accum_out=sums[:, j, c : c + 1],
            )

        def gains():
            nc.vector.tensor_copy(out=g1f[:], in_=g1b[:].rearrange("p g t -> p (g t)"))

        def signs(k):
            rs = slice(2 * k, 2 * k + 2)
            nc.vector.tensor_scalar(
                out=yh[:, rs, :], in0=ut[:, rs, :], scalar1=0.0, scalar2=0.5, op0=ALU.is_ge, op1=ALU.subtract
            )

        def early_sum():
            nc.vector.reduce_sum(out=part[:], in_=sums[:, :, 0:3], axis=AX.X)

        def early_mean():
            nc.vector.tensor_scalar(out=part[:], in0=part[:], scalar1=1.0 / B, scalar2=None, op0=ALU.mult)

        def means(cg):
            js = slice(4 * cg, 4 * cg + 4)
            nc.vector.scalar_tensor_tensor(
                out=mean[:, js], in0=sums[:, js, 3], scalar=1.0 / B, in1=part[:, js], op0=ALU.mult, op1=ALU.add
            )

        def shifts(cg):
            js = slice(4 * cg, 4 * cg + 4)
            nc.vector.scalar_tensor_tensor(
                out=shift[:, js], in0=mean[:, js], scalar=-1.0, in1=g1f[:, js], op0=ALU.mult, op1=ALU.mult
            )

        def centre_v(cg, h, t):
            j = 4 * cg + t
            cols = slice(512 * h, 512 * h + 512)
            nc.vector.tensor_scalar(
                out=hp[:, j, cols], in0=r32[:, j, cols], scalar1=mean[:, j : j + 1], scalar2=g1f[:, j : j + 1],
                op0=ALU.subtract, op1=ALU.mult,
            )

        def centre_s(cg, h, t):
            j = 4 * cg + t
            cols = slice(512 * h, 512 * h + 512)
            nc.scalar.activation(
                out=hp[:, j, cols], in_=r32[:, j, cols], func=ACT.Identity, scale=g1f[:, j : j + 1],
                bias=shift[:, j : j + 1],
            )

        hi = {}

        def weave(cg, blk):
            hi[cg, blk] = keep.tile([P, 1024], BF16, align_bytes=64, name="hi%d%d" % (cg, blk))
            dst = hi[cg, blk][:].rearrange("p (c i t) -> p c t i", i=4, t=4)
            src = hp[:, 4 * cg : 4 * cg + 4, 256 * blk : 256 * blk + 256].rearrange("p t (c i) -> p c t i", i=4)
            return dst, src

        def weave_v(cg, blk):
            dst, src = weave(cg, blk)
            nc.vector.tensor_copy(out=dst, in_=src)

        def weave_s(cg, blk):
            dst, src = weave(cg, blk)
            nc.scalar.copy(out=dst, in_=src)

        def quant_h(cg, blk):
            cols = slice(256 * blk, 256 * blk + 256)
            nc.vector.quantize_mx(out=hc[:, cg, cols].bitcast(FP8X4), scales=hs[:, cg, cols], in_=hi[cg, blk][:])

        def mm2(bank, codes, scales, b, n, first, last):
            for g in range(KG):
                nc.tensor.matmul_mx(
                    out=bank[:],
                    lhsT=codes[:, g, 128 * b : 128 * b + 128].bitcast(FP8X4),
                    lhsT_scale=scales[:, g, 128 * b : 128 * b + 128],
                    rhs=w2[n][:, g, :].bitcast(FP8X4),
                    rhs_scale=w2s[n][4 * g : P, :],
                    start=(first and g == 0),
                    stop=(last and g == KG - 1),
                )

        def px(b):
            mm2(take(("p", b)), xc, xs, b, "x", True, False)

        def wh(b):
            mm2(held["p", b][1], hc, hs, b, "h", False, True)

        def sv(b):
            mm2(take(("s", b)), hc, hs, b, "v", True, True)

        th = {}
        qq = {}
        ww = {}
        ee = {}

        def tanh(b):
            th[b] = work.tile([P, C], F32, align_bytes=64, name="tht")
            nc.scalar.activation(out=th[b][:], in_=give(("p", b))[:], func=ACT.Tanh)

        def add(b, c0=0, c1=C):
            qq[b, c0] = work.tile([P, C], F32, align_bytes=64, name="qt")
            bank = give(("s", b)) if c1 == C else held["s", b][1]
            nc.vector.tensor_tensor(
                out=qq[b, c0][:, : c1 - c0], in0=bank[:, c0:c1], in1=th[b][:, c0:c1], op=ALU.add
            )

        def mult(b, c0=0, c1=C):
            ww[b, c0] = work.tile([P, C], F32, align_bytes=64, name="wt")
            nc.vector.tensor_tensor(
                out=ww[b, c0][:, : c1 - c0], in0=qq[b, c0][:, : c1 - c0], in1=yh[:, b, c0:c1], op=ALU.mult
            )

        def mult_g(b):
            ww[b, 0] = work.tile([P, C], F32, align_bytes=64, name="wt")
            nc.gpsimd.tensor_tensor(out=ww[b, 0][:], in0=qq[b, 0][:], in1=yh[:, b, :], op=ALU.mult)

        def expo(b, c0=0, c1=C):
            n = c1 - c0
            ee[b, c0] = work.tile([P, C], F32, align_bytes=64, name="et")
            nc.scalar.activation(
                out=ee[b, c0][:, :n], in_=ww[b, c0][:, :n], func=ACT.Exp, scale=-1.6, bias=math.log(2.0)
            )

        ov = out.rearrange("(p r) c -> p r c", r=RT)

        def finish(b, c0=0, c1=C):
            n = c1 - c0
            o = work.tile([P, C], F32, align_bytes=64, name="ot")
            nc.vector.scalar_tensor_tensor(
                out=o[:, :n], in0=ee[b, c0][:, :n], scalar=2.0, in1=yh[:, b, c0:c1], op0=ALU.add, op1=ALU.mult
            )
            nc.sync.dma_start(out=ov[:, b, c0:c1], in_=o[:, :n])

        spread_pe(0)
        spread_pe(1)
        spread_s(0)
        permute_scales()
        spread_s(1)
        product(0, 0, 512)
        product(0, 512, D)
        product(1)
        turn(0)
        copy_x(0)
        permute(0)
        turn(1)
        permute(1)
        copy_x(1)
        quant_x(0)
        product(2)
        mm1(0, 0)
        mm1(0, 1)
        relu_s(0, 0)
        mm1(0, 2)
        product(3)
        relu_s(0, 1)
        mm1(0, 3)
        mm1(0, 4)
        relu_s(0, 2)
        mm1(0, 5)
        relu_s(0, 3)
        turn(2)
        relu_s(0, 4)
        product(4)
        relu_s(0, 5)
        turn(3)
        copy_x(2)
        mm1(0, 6)
        product(5)
        copy_x(3)
        mm1(0, 7)
        turn(4)
        relu_s(0, 6)
        relu_s(0, 7)
        quant_x(1)
        turn(5)
        copy_x(4)
        product(6)
        mm1(1, 0)
        copy_x(5)
        mm1(1, 1)
        relu_s(1, 0)
        mm1(1, 2)
        gains()
        mm1(1, 3)
        product(7)
        relu_s(1, 1)
        mm1(1, 4)
        relu_s(1, 2)
        mm1(1, 5)
        relu_s(1, 3)
        mm1(1, 6)
        relu_s(1, 4)
        turn(6)
        signs(0)
        relu_s(1, 5)
        quant_x(2)
        turn(7)
        relu_s(1, 6)
        copy_x(6)
        mm1(1, 7)
        mm1(2, 0)
        copy_x(7)
        relu_v(1, 7)
        mm1(2, 1)
        mm1(2, 2)
        relu_s(2, 0)
        quant_x(3)
        mm1(2, 3)
        relu_s(2, 1)
        mm1(2, 4)
        relu_s(2, 2)
        mm1(2, 5)
        relu_s(2, 3)
        mm1(2, 6)
        mm1(2, 7)
        relu_s(2, 4)
        mm1(3, 0)
        relu_s(2, 5)
        relu_v(2, 7)
        mm1(3, 1)
        relu_s(2, 6)
        mm1(3, 5)
        signs(1)
        relu_s(3, 0)
        mm1(3, 2)
        early_sum()
        mm1(3, 3)
        relu_s(3, 1)
        early_mean()
        relu_v(3, 5)
        mm1(3, 6)
        relu_s(3, 2)
        mm1(3, 4)
        relu_s(3, 3)
        relu_v(3, 6)
        mm1(3, 7)
        relu_s(3, 4)
        px(0)
        means(0)
        relu_v(3, 7)
        px(1)
        shifts(0)
        centre_v(0, 0, 0)
        centre_s(0, 0, 3)
        means(1)
        centre_v(0, 0, 1)
        px(2)
        shifts(1)
        centre_v(0, 0, 2)
        px(3)
        centre_s(1, 0, 3)
        centre_v(1, 0, 0)
        centre_v(1, 0, 1)
        px(4)
        weave_s(0, 1)
        centre_v(1, 0, 2)
        weave_v(0, 0)
        weave_v(1, 0)
        weave_s(1, 1)
        quant_h(0, 0)
        quant_h(1, 0)
        centre_s(0, 1, 3)
        centre_v(0, 1, 0)
        wh(0)
        centre_v(0, 1, 1)
        centre_s(1, 1, 3)
        centre_v(0, 1, 2)
        sv(0)
        quant_h(0, 1)
        tanh(0)
        quant_h(1, 1)
        wh(1)
        centre_v(1, 1, 0)
        weave_s(0, 2)
        sv(1)
        signs(2)
        centre_v(1, 1, 1)
        wh(2)
        centre_v(1, 1, 2)
        add(0)
        tanh(1)
        sv(2)
        quant_h(0, 2)
        wh(3)
        weave_s(1, 2)
        mult(0)
        sv(3)
        add(1)
        tanh(2)
        quant_h(1, 2)
        signs(3)
        tanh(3)
        wh(4)
        add(2)
        mult_g(1)
        expo(0)
        sv(4)
        add(3)
        weave_s(0, 3)
        px(5)
        finish(0)
        px(6)
        mult(2)
        px(7)
        tanh(4)
        mult_g(3)
        wh(5)
        weave_s(1, 3)
        add(4)
        sv(5)
        mult(4)
        expo(1)
        quant_h(0, 3)
        quant_h(1, 3)
        expo(2)
        finish(1)
        wh(6)
        tanh(5)
        finish(2)
        sv(6)
        expo(3)
        add(5)
        wh(7)
        expo(4)
        finish(3)
        sv(7)
        tanh(6)
        finish(4)
        tanh(7)
        add(6)
        mult_g(5)
        add(7, 0, HALF)
        add(7, HALF, C)
        mult(6)
        expo(5)
        mult(7, 0, HALF)
        expo(6)
        finish(5)
        expo(7, 0, HALF)
        mult(7, HALF, C)
        finish(6)
        expo(7, HALF, C)
        finish(7, 0, HALF)
        finish(7, HALF, C)
